import numpy as np
import ml_dtypes


def mxq(x, axis, fmt="e4m3"):
    dtype, down = {"e4m3": (ml_dtypes.float8_e4m3fn, 7), "e5m2": (ml_dtypes.float8_e5m2, 14)}[fmt]
    v = np.moveaxis(np.asarray(x, np.float32).astype(ml_dtypes.bfloat16).astype(np.float64), axis, -1)
    blocks = v.reshape(v.shape[:-1] + (-1, 32))
    amax = np.abs(blocks).max(-1, keepdims=True)
    byte = np.maximum(np.where(amax > 0, np.frexp(amax)[1] - 1 + 127, 0) - down, 1)
    scale = np.exp2(byte - 127.0)
    codes = (blocks / scale).astype(np.float32).astype(dtype).astype(np.float64)
    return np.moveaxis((codes * scale).reshape(v.shape), -1, axis)


WIDE = False


def mx_kscale(k):
    if not WIDE:
        return np.ones(k)
    levels = np.array([10, -10, 5, -5, 0])
    if k % 512:
        return np.exp2(np.random.permutation(np.resize(levels, k // 32))).repeat(32)
    a = np.empty((k // 512, 16))
    for p in range(k // 512):
        a[p, :8] = np.random.permutation(np.resize(levels, 8))
        for g in range(8):
            far = levels[np.abs(levels - a[p, g]) >= 10]
            a[p, g + 8] = far[np.random.randint(len(far))]
    return np.exp2(a.ravel()).repeat(32)


def f64(x):
    return np.asarray(x).astype(np.float64)


def striped8(idx):
    return np.asarray(idx).reshape(8, -1, 16).transpose(0, 2, 1).reshape(128, -1).astype(np.uint16)


def unstriped8(offs):
    return offs.reshape(8, 16, -1).transpose(0, 2, 1).reshape(8, -1).astype(np.int64)


def pick8(x, idx, run):
    r = np.arange(len(x))
    return x[r[:, None], idx[r % (8 * run) // run]]


E2M1 = np.array([0.0, 0.5, 1.0, 1.5, 2.0, 3.0, 4.0, 6.0, -0.0, -0.5, -1.0, -1.5, -2.0, -3.0, -4.0, -6.0])


def pack_weight(w, fmt):
    k, n = w.shape
    w = f64(np.asarray(w, np.float32).astype(ml_dtypes.bfloat16)).reshape(k // 32, 32, n)
    amax = np.abs(w).max(1)
    if fmt == "e4m3":
        byte = np.frexp(amax)[1] - 1 + 127 - 7
    else:
        mant, ex = np.frexp(amax / 6.0)
        byte = np.where(mant > 0.5, ex, ex - 1) + 127
    byte = np.clip(np.where(amax > 0, byte, 1), 1, 254)
    scaled = (w * np.exp2(127.0 - byte)[:, None, :]).reshape(k, n).astype(np.float32)
    by_word = np.ascontiguousarray(scaled.reshape(k // 512, 128, 4, n).transpose(0, 1, 3, 2))
    if fmt == "e4m3":
        words = by_word.astype(ml_dtypes.float8_e4m3fn).view(np.uint8)
    else:
        c = by_word.astype(ml_dtypes.float4_e2m1fn).view(np.uint8) & 0xF
        words = (c[..., 0::2] | (c[..., 1::2] << 4)).reshape(k // 512, 128, 2 * n)
    return np.ascontiguousarray(words), np.ascontiguousarray(byte.astype(np.uint8).reshape(k // 512, 16, n))


def unpack_weight(words, scales, fmt):
    g, _, n = scales.shape
    words = np.ascontiguousarray(words).reshape(g, 128, n, -1)
    if fmt == "e4m3":
        vals = words.view(ml_dtypes.float8_e4m3fn).astype(np.float64)
    else:
        nib = np.empty((g, 128, n, 4), np.uint8)
        nib[..., 0::2] = words & 0xF
        nib[..., 1::2] = words >> 4
        vals = E2M1[nib]
    vals = vals * np.repeat(np.exp2(scales.astype(np.float64) - 127.0), 8, axis=1)[..., None]
    return vals.transpose(0, 1, 3, 2).reshape(g * 512, n)


def softplus(v):
    return np.log(1.0 + np.exp(v))


def sigmoid(v):
    return 1.0 / (1.0 + np.exp(-v))


D, E, T, Q, I = 512, 512, 1024, 128, 512


def setup_inputs():
    n = np.random.standard_normal
    idx = np.stack([np.random.permutation(T)[:I] for _ in range(8)])
    fd = mx_kscale(D)
    fe = mx_kscale(E)
    keysp = pack_weight(n((D, T)) / fd[:, None], "e4m3")
    return {
        "query": (n((D, Q)) * 1.0 / np.sqrt(D) * fd[:, None]).astype(np.float32),
        "keys_words": keysp[0],
        "keys_scales": keysp[1],
        "gout": (n((E, Q)) * 1 / np.sqrt(E) * fe[:, None]).astype(np.float32),
        "vals": (n((E, T)) / fe[:, None]).astype(np.float32),
        "th": (np.random.uniform(-0.5, 0.5, (Q, 1))).astype(np.float32),
        "reserve": (np.random.uniform(20.0, 60.0, (Q, 1))).astype(np.float32),
        "dquery": (n((D, Q)) * 1.0 / np.sqrt(D) * fd[:, None]).astype(np.float32),
        "base": (0.5 * n((Q, T))).astype(np.float32),
        "offs": striped8(idx),
    }


def reference(query, keys_words, keys_scales, gout, vals, th, reserve, dquery, base, offs):
    idx = unstriped8(offs)
    keysu = unpack_weight(keys_words, keys_scales, "e4m3")
    queryq = mxq(f64(query), 0, "e4m3")
    a = queryq.T @ keysu
    dqueryq = mxq(f64(dquery), 0, "e4m3")
    ta = dqueryq.T @ keysu
    p = softplus(pick8(a, idx, 16) - f64(th))
    z = np.sum(p, axis=1, keepdims=True) + f64(reserve)
    goutq = mxq(f64(gout), 0, "e4m3")
    valsq = mxq(f64(vals), 0, "e4m3")
    c0 = goutq.T @ valsq
    dw = pick8(c0, idx, 16)
    dz = np.sum(dw * p / np.square(z) * (-1.0), axis=1, keepdims=True)
    dp = dw / z + dz
    xp = pick8(ta, idx, 16) * sigmoid(pick8(a, idx, 16) - f64(th))
    xz = np.sum(xp, axis=1, keepdims=True)
    xdz = np.sum((xp * dw - xz * z * 2.0 * dw * p / np.square(z)) / np.square(z) * (-1.0), axis=1, keepdims=True)
    xdp = xz * dw / np.square(z) * (-1.0) + xdz
    xe1 = xdp * sigmoid(pick8(a, idx, 16) - f64(th)) + pick8(ta, idx, 16) * sigmoid(pick8(a, idx, 16) - f64(th)) * (1.0 - sigmoid(pick8(a, idx, 16) - f64(th))) * dp
    xs1 = np.zeros((Q, T))
    xs1[np.arange(Q)[:, None], idx[np.arange(Q) % 128 // 16]] = xe1
    y = xs1 * 1024.0 + f64(base)
    return y

@@ -1,0 +1,161 @@
+from contextlib import ExitStack
+
+import concourse.mybir as mybir
+
+D, E, T, Q, I = 512, 512, 1024, 128, 512
+FLOPS = 3 * 2 * D * Q * T
+
+F32 = mybir.dt.float32
+BF16 = mybir.dt.bfloat16
+I32 = mybir.dt.int32
+U32 = mybir.dt.uint32
+U16 = mybir.dt.uint16
+U8 = mybir.dt.uint8
+FP8X4 = mybir.dt.float8_e4m3fn_x4
+ALU = mybir.AluOpType
+ACT = mybir.ActivationFunctionType
+
+P = 128
+PACK = 4
+BANK = 512
+CHUNK = 256
+CLAMP = 16.0
+
+
+def tile_attend_hvspotlight_heads_kernel(tc, query, keys_words, keys_scales, gout, vals, th, reserve, dquery, base, offs, out):
+    nc = tc.nc
+    with ExitStack() as ctx:
+        sb = ctx.enter_context(tc.tile_pool(name="sb", bufs=1))
+        ps = ctx.enter_context(tc.psum_pool(name="ps", bufs=1))
+
+        def load_rows(name, rows):
+            raw = sb.tile([P, PACK, rows.shape[1]], F32, name=name + "_raw")
+            nc.sync.dma_start(out=raw[:], in_=rows.rearrange("(p j) w -> p j w", j=PACK))
+            return raw
+
+        def interleave(name, raw, on_vector):
+            width = raw.shape[2]
+            grouped = sb.tile([P, width, PACK], BF16, name=name + "_bf", align_bytes=64)
+            dst = grouped[:].rearrange("p (c i) j -> p c j i", i=4)
+            src = raw[:].rearrange("p j (c i) -> p c j i", i=4)
+            if on_vector:
+                nc.vector.tensor_copy(out=dst, in_=src)
+            else:
+                nc.scalar.copy(out=dst, in_=src)
+            return grouped
+
+        def quantize(name, grouped):
+            width = grouped.shape[1]
+            codes = sb.tile([P, width], U32, name=name + "_codes", align_bytes=64)
+            scales = sb.tile([P, width], U8, name=name + "_scales", align_bytes=64)
+            nc.vector.quantize_mx(out=codes[:].bitcast(FP8X4), scales=scales[:], in_=grouped[:].rearrange("p w j -> p (w j)"))
+            return codes, scales
+
+        def product(name, lhs, rhs_codes, rhs_scales):
+            acc = ps.tile([P, rhs_codes.shape[1]], F32, name=name)
+            nc.tensor.matmul_mx(out=acc[:], lhsT=lhs[0][:].bitcast(FP8X4), lhsT_scale=lhs[1][:],
+                                rhs=rhs_codes.bitcast(FP8X4), rhs_scale=rhs_scales, start=True, stop=True)
+            return acc
+
+        k_scales = sb.tile([P, T], U8, name="k_scales", align_bytes=64)
+        nc.vector.memset(k_scales[:].bitcast(I32), 0)
+        warm = sb.tile([P, 2], F32, name="warm")
+        nc.vector.memset(warm[:, 0:1], 0.0)
+        placed = sb.tile([P, T], F32, name="placed")
+        nc.vector.memset(placed[:], 0.0)
+
+        q_raw = load_rows("q", query)
+        k_words = keys_words[0].rearrange("p n t -> p (n t)").bitcast(I32)
+        k_codes = []
+        for h in range(2):
+            half = sb.tile([P, BANK], U32, name="k_codes%d" % h, align_bytes=64)
+            nc.sync.dma_start(out=half[:].bitcast(I32), in_=k_words[:, h * BANK : (h + 1) * BANK])
+            k_codes.append(half)
+        for g in range(4):
+            nc.scalar.dma_start(out=k_scales[32 * g : 32 * g + 4, :].bitcast(I32), in_=keys_scales[0, 4 * g : 4 * g + 4, :].bitcast(I32))
+        nc.scalar.activation(out=warm[:, 1:2], in_=warm[:, 0:1], func=ACT.Sigmoid)
+        dq_raw = load_rows("dq", dquery)
+        offsets = sb.tile([P, I // 16], U16, name="offsets")
+        nc.sync.dma_start(offsets[:], offs)
+        th_sb = sb.tile([P, 1], F32, name="th_sb")
+        nc.gpsimd.dma_start(out=th_sb[:], in_=th)
+        res_sb = sb.tile([P, 1], F32, name="res_sb")
+        nc.gpsimd.dma_start(out=res_sb[:], in_=reserve)
+        v_raw = [load_rows("v0", vals[:, 0:CHUNK])]
+        g_raw = load_rows("g", gout)
+        v_raw.extend([load_rows("v%d" % c, vals[:, c * CHUNK : (c + 1) * CHUNK]) for c in range(1, T // CHUNK)])
+        base_sb = sb.tile([P, T], F32, name="base_sb")
+        nc.sync.dma_start(out=base_sb[:], in_=base)
+
+        q_mx = quantize("q", interleave("q", q_raw, True))
+        a_sb = sb.tile([P, T], F32, name="a_sb")
+        a_ps = [product("a_ps%d" % h, q_mx, k_codes[h][:], k_scales[:, h * BANK : (h + 1) * BANK]) for h in range(2)]
+        nc.scalar.copy(out=a_sb[:, 0:BANK], in_=a_ps[0][:])
+        nc.vector.tensor_copy(out=a_sb[:, BANK:T], in_=a_ps[1][:])
+        neg_a = sb.tile([P, I], F32, name="neg_a")
+        nc.vector.tensor_scalar(neg_a[:], a_sb[:].indirect(offsets[:]), -1.0, 0.0, ALU.mult, ALU.add)
+        neg_u = sb.tile([P, I], F32, name="neg_u")
+        nc.vector.tensor_scalar(neg_u[:], neg_a[:], th_sb[:], -CLAMP, ALU.add, ALU.max)
+        sm = sb.tile([P, I], F32, name="sm")
+        nc.scalar.activation(out=sm[:], in_=neg_u[:], func=ACT.Sigmoid)
+        ln_sm = sb.tile([P, I], F32, name="ln_sm")
+        nc.scalar.activation(out=ln_sm[:], in_=sm[:], func=ACT.Ln)
+
+        dq_mx = quantize("dq", interleave("dq", dq_raw, True))
+        ta_sb = sb.tile([P, T], F32, name="ta_sb")
+        for h in range(2):
+            acc = product("ta_ps%d" % h, dq_mx, k_codes[h][:], k_scales[:, h * BANK : (h + 1) * BANK])
+            nc.scalar.copy(out=ta_sb[:, h * BANK : (h + 1) * BANK], in_=acc[:])
+
+        c_sb = sb.tile([P, T], F32, name="c_sb")
+        v_bf = [interleave("v0", v_raw[0], True)]
+        g_bf = interleave("g", g_raw, True)
+        t = sb.tile([P, I], F32, name="t")
+        nc.vector.tensor_copy(t[:], ta_sb[:].indirect(offsets[:]))
+        g_mx = quantize("g", g_bf)
+        v_bf.extend([interleave("v%d" % c, v_raw[c], c < 2) for c in range(1, T // CHUNK)])
+        for c in range(T // CHUNK):
+            v_mx = quantize("v%d" % c, v_bf[c])
+            acc = product("c_ps%d" % c, g_mx, v_mx[0][:], v_mx[1][:])
+            nc.scalar.copy(out=c_sb[:, c * CHUNK : (c + 1) * CHUNK], in_=acc[:])
+
+        neg_xp = sb.tile([P, I], F32, name="neg_xp")
+        neg_xz = sb.tile([P, 1], F32, name="neg_xz")
+        nc.vector.scalar_tensor_tensor(neg_xp[:], sm[:], 1.0, t[:], ALU.subtract, ALU.mult, accum_out=neg_xz[:])
+        neg_p = sb.tile([P, I], F32, name="neg_p")
+        neg_sum = sb.tile([P, 1], F32, name="neg_sum")
+        z = sb.tile([P, 1], F32, name="z")
+        r = sb.tile([P, 1], F32, name="r")
+        neg_xzr = sb.tile([P, 1], F32, name="neg_xzr")
+        gain = sb.tile([P, 1], F32, name="gain")
+        nc.vector.scalar_tensor_tensor(neg_p[:], neg_a[:], th_sb[:], ln_sm[:], ALU.add, ALU.min, accum_out=neg_sum[:])
+        nc.vector.tensor_scalar(z[:], neg_sum[:], -1.0, res_sb[:], ALU.mult, ALU.add)
+        nc.vector.reciprocal(r[:], z[:])
+        nc.vector.tensor_scalar(neg_xzr[:], neg_xz[:], r[:], None, ALU.mult)
+        nc.vector.tensor_scalar(gain[:], r[:], -1024.0, None, ALU.mult)
+        hx = sb.tile([P, I], F32, name="hx")
+        nc.vector.scalar_tensor_tensor(hx[:], t[:], neg_xzr[:], neg_xp[:], ALU.add, ALU.add)
+        neg_s = sb.tile([P, I], F32, name="neg_s")
+        nc.scalar.activation(out=neg_s[:], in_=sm[:], func=ACT.Copy, bias=-1.0)
+
+        w = sb.tile([P, I], F32, name="w")
+        nc.vector.tensor_copy(w[:], c_sb[:].indirect(offsets[:]))
+        wp = sb.tile([P, I], F32, name="wp")
+        neg_r1 = sb.tile([P, 1], F32, name="neg_r1")
+        nc.vector.scalar_tensor_tensor(wp[:], w[:], r[:], neg_p[:], ALU.mult, ALU.mult, accum_out=neg_r1[:])
+        wx = sb.tile([P, I], F32, name="wx")
+        neg_r2 = sb.tile([P, 1], F32, name="neg_r2")
+        nc.vector.scalar_tensor_tensor(wx[:], w[:], r[:], neg_xp[:], ALU.mult, ALU.mult, accum_out=neg_r2[:])
+        y0 = sb.tile([P, I], F32, name="y0")
+        nc.vector.scalar_tensor_tensor(y0[:], w[:], neg_r1[:], hx[:], ALU.add, ALU.mult)
+        shift = sb.tile([P, 1], F32, name="shift")
+        nc.vector.tensor_scalar(shift[:], neg_r1[:], neg_xzr[:], neg_r2[:], ALU.mult, ALU.add)
+        y = sb.tile([P, I], F32, name="y")
+        nc.vector.tensor_scalar(y[:], y0[:], shift[:], gain[:], ALU.add, ALU.mult)
+        nc.vector.tensor_tensor(placed[:].indirect(offsets[:]), y[:], neg_s[:], ALU.mult)
+
+        for h in range(4):
+            cols = slice(h * CHUNK, (h + 1) * CHUNK)
+            res = sb.tile([P, CHUNK], F32, name="res%d" % h)
+            nc.vector.tensor_tensor(res[:], placed[:, cols], base_sb[:, cols], ALU.add)
+            (nc.sync if h % 2 == 0 else nc.scalar).dma_start(out=out[:, cols], in_=res[:])

@@ -19,7 +19,9 @@ P = 128
 PACK = 4
 BANK = 512
 CHUNK = 256
-CLAMP = 16.0
+FLOOR = 2.0 ** -50
+RUN = 2
+SHARE = 96
 
 
 def tile_attend_hvspotlight_heads_kernel(tc, query, keys_words, keys_scales, gout, vals, th, reserve, dquery, base, offs, out):
@@ -28,21 +30,32 @@ def tile_attend_hvspotlight_heads_kernel(tc, query, keys_words, keys_scales, gou
         sb = ctx.enter_context(tc.tile_pool(name="sb", bufs=1))
         ps = ctx.enter_context(tc.psum_pool(name="ps", bufs=1))
 
+        def column(name):
+            return sb.tile([P, 1], F32, name=name)
+
+        def slots(name, tag=""):
+            return sb.tile([P, I], F32, name=name, tag=tag or name, align_bytes=64)
+
         def load_rows(name, rows):
-            raw = sb.tile([P, PACK, rows.shape[1]], F32, name=name + "_raw")
+            raw = sb.tile([P, PACK, rows.shape[1]], F32, name=name + "_raw", tag=name + "_raw", align_bytes=64)
             nc.sync.dma_start(out=raw[:], in_=rows.rearrange("(p j) w -> p j w", j=PACK))
             return raw
 
-        def interleave(name, raw, on_vector):
-            width = raw.shape[2]
-            grouped = sb.tile([P, width, PACK], BF16, name=name + "_bf", align_bytes=64)
-            dst = grouped[:].rearrange("p (c i) j -> p c j i", i=4)
-            src = raw[:].rearrange("p j (c i) -> p c j i", i=4)
+        def grouped_tile(name, width):
+            return sb.tile([P, width, PACK], BF16, name=name + "_bf", tag=name + "_bf", align_bytes=64)
+
+        def interleave(grouped, raw, on_vector):
+            dst = grouped.rearrange("p (c i) j -> p c j i", i=RUN)
+            src = raw.rearrange("p j (c i) -> p c j i", i=RUN)
             if on_vector:
                 nc.vector.tensor_copy(out=dst, in_=src)
             else:
                 nc.scalar.copy(out=dst, in_=src)
-            return grouped
+
+        def vector_operand(name, raw):
+            grouped = grouped_tile(name, raw.shape[2])
+            interleave(grouped[:], raw, True)
+            return quantize(name, grouped)
 
         def quantize(name, grouped):
             width = grouped.shape[1]
@@ -51,8 +64,8 @@ def tile_attend_hvspotlight_heads_kernel(tc, query, keys_words, keys_scales, gou
             nc.vector.quantize_mx(out=codes[:].bitcast(FP8X4), scales=scales[:], in_=grouped[:].rearrange("p w j -> p (w j)"))
             return codes, scales
 
-        def product(name, lhs, rhs_codes, rhs_scales):
-            acc = ps.tile([P, rhs_codes.shape[1]], F32, name=name)
+        def product(bank, lhs, rhs_codes, rhs_scales):
+            acc = ps.tile([P, rhs_codes.shape[1]], F32, name=bank)
             nc.tensor.matmul_mx(out=acc[:], lhsT=lhs[0][:].bitcast(FP8X4), lhsT_scale=lhs[1][:],
                                 rhs=rhs_codes.bitcast(FP8X4), rhs_scale=rhs_scales, start=True, stop=True)
             return acc
@@ -64,6 +77,8 @@ def tile_attend_hvspotlight_heads_kernel(tc, query, keys_words, keys_scales, gou
         placed = sb.tile([P, T], F32, name="placed")
         nc.vector.memset(placed[:], 0.0)
 
+        for g in range(4):
+            (nc.scalar if g < 2 else nc.sync).dma_start(out=k_scales[32 * g : 32 * g + 4, :].bitcast(I32), in_=keys_scales[0, 4 * g : 4 * g + 4, :].bitcast(I32))
         q_raw = load_rows("q", query)
         k_words = keys_words[0].rearrange("p n t -> p (n t)").bitcast(I32)
         k_codes = []
@@ -71,91 +86,89 @@ def tile_attend_hvspotlight_heads_kernel(tc, query, keys_words, keys_scales, gou
             half = sb.tile([P, BANK], U32, name="k_codes%d" % h, align_bytes=64)
             nc.sync.dma_start(out=half[:].bitcast(I32), in_=k_words[:, h * BANK : (h + 1) * BANK])
             k_codes.append(half)
-        for g in range(4):
-            nc.scalar.dma_start(out=k_scales[32 * g : 32 * g + 4, :].bitcast(I32), in_=keys_scales[0, 4 * g : 4 * g + 4, :].bitcast(I32))
-        nc.scalar.activation(out=warm[:, 1:2], in_=warm[:, 0:1], func=ACT.Sigmoid)
         dq_raw = load_rows("dq", dquery)
+        nc.scalar.activation(out=warm[:, 1:2], in_=warm[:, 0:1], func=ACT.Sigmoid)
+        th_sb = column("th_sb")
+        nc.gpsimd.dma_start(out=th_sb[:], in_=th)
+        res_sb = column("res_sb")
+        nc.gpsimd.dma_start(out=res_sb[:], in_=reserve)
+        g_raw = load_rows("g", gout)
         offsets = sb.tile([P, I // 16], U16, name="offsets")
         nc.sync.dma_start(offsets[:], offs)
-        th_sb = sb.tile([P, 1], F32, name="th_sb")
-        nc.gpsimd.dma_start(out=th_sb[:], in_=th)
-        res_sb = sb.tile([P, 1], F32, name="res_sb")
-        nc.gpsimd.dma_start(out=res_sb[:], in_=reserve)
-        v_raw = [load_rows("v0", vals[:, 0:CHUNK])]
-        g_raw = load_rows("g", gout)
-        v_raw.extend([load_rows("v%d" % c, vals[:, c * CHUNK : (c + 1) * CHUNK]) for c in range(1, T // CHUNK)])
+        v_raw = [load_rows("v%d" % c, vals[:, c * CHUNK : (c + 1) * CHUNK]) for c in range(T // CHUNK)]
         base_sb = sb.tile([P, T], F32, name="base_sb")
         nc.sync.dma_start(out=base_sb[:], in_=base)
 
-        q_mx = quantize("q", interleave("q", q_raw, True))
+        q_mx = vector_operand("q", q_raw[:])
         a_sb = sb.tile([P, T], F32, name="a_sb")
-        a_ps = [product("a_ps%d" % h, q_mx, k_codes[h][:], k_scales[:, h * BANK : (h + 1) * BANK]) for h in range(2)]
-        nc.scalar.copy(out=a_sb[:, 0:BANK], in_=a_ps[0][:])
-        nc.vector.tensor_copy(out=a_sb[:, BANK:T], in_=a_ps[1][:])
-        neg_a = sb.tile([P, I], F32, name="neg_a")
-        nc.vector.tensor_scalar(neg_a[:], a_sb[:].indirect(offsets[:]), -1.0, 0.0, ALU.mult, ALU.add)
-        neg_u = sb.tile([P, I], F32, name="neg_u")
-        nc.vector.tensor_scalar(neg_u[:], neg_a[:], th_sb[:], -CLAMP, ALU.add, ALU.max)
-        sm = sb.tile([P, I], F32, name="sm")
-        nc.scalar.activation(out=sm[:], in_=neg_u[:], func=ACT.Sigmoid)
-        ln_sm = sb.tile([P, I], F32, name="ln_sm")
-        nc.scalar.activation(out=ln_sm[:], in_=sm[:], func=ACT.Ln)
-
-        dq_mx = quantize("dq", interleave("dq", dq_raw, True))
+        for c in range(T // CHUNK):
+            cols = slice(c * CHUNK, (c + 1) * CHUNK)
+            acc = product("quarter%d" % c, q_mx, k_codes[c // 2][:, (c % 2) * CHUNK : (c % 2 + 1) * CHUNK], k_scales[:, cols])
+            nc.scalar.copy(out=a_sb[:, cols], in_=acc[:])
+        dq_mx = vector_operand("dq", dq_raw[:])
         ta_sb = sb.tile([P, T], F32, name="ta_sb")
         for h in range(2):
-            acc = product("ta_ps%d" % h, dq_mx, k_codes[h][:], k_scales[:, h * BANK : (h + 1) * BANK])
+            acc = product("half%d" % h, dq_mx, k_codes[h][:], k_scales[:, h * BANK : (h + 1) * BANK])
             nc.scalar.copy(out=ta_sb[:, h * BANK : (h + 1) * BANK], in_=acc[:])
 
-        c_sb = sb.tile([P, T], F32, name="c_sb")
-        v_bf = [interleave("v0", v_raw[0], True)]
-        g_bf = interleave("g", g_raw, True)
-        t = sb.tile([P, I], F32, name="t")
+        neg_a = slots("neg_a")
+        nc.vector.tensor_scalar(neg_a[:], a_sb[:].indirect(offsets[:]), -1.0, 0.0, ALU.mult, ALU.add)
+        pieces = [(0, CHUNK), (CHUNK, CHUNK), (2 * CHUNK, CHUNK), (3 * CHUNK, P), (3 * CHUNK + P, P)]
+        v_bf = [grouped_tile("v%d" % c, pieces[c][1]) for c in range(5)]
+        interleave(v_bf[0][:], v_raw[0][:], False)
+        sm = slots("sm")
+        nc.scalar.activation(out=sm[:], in_=neg_a[:], func=ACT.Sigmoid, bias=th_sb[:])
+        interleave(v_bf[1][:, 0:SHARE, :], v_raw[1][:, :, 0:SHARE], False)
+
+        t = slots("t")
         nc.vector.tensor_copy(t[:], ta_sb[:].indirect(offsets[:]))
-        g_mx = quantize("g", g_bf)
-        v_bf.extend([interleave("v%d" % c, v_raw[c], c < 2) for c in range(1, T // CHUNK)])
-        for c in range(T // CHUNK):
+        g_mx = vector_operand("g", g_raw[:])
+        interleave(v_bf[1][:, SHARE:CHUNK, :], v_raw[1][:, :, SHARE:CHUNK], True)
+        ln_sm = slots("ln_sm", "v1_raw")
+        nc.scalar.activation(out=ln_sm[:], in_=sm[:], func=ACT.Ln, bias=FLOOR)
+        interleave(v_bf[2][:], v_raw[2][:], True)
+        interleave(v_bf[3][:], v_raw[3][:, :, 0:P], True)
+        interleave(v_bf[4][:], v_raw[3][:, :, P:CHUNK], True)
+        c_sb = sb.tile([P, T], F32, name="c_sb")
+        banks = ["quarter0", "quarter1", "quarter2", "quarter3", "half0"]
+        for c in range(5):
             v_mx = quantize("v%d" % c, v_bf[c])
-            acc = product("c_ps%d" % c, g_mx, v_mx[0][:], v_mx[1][:])
-            nc.scalar.copy(out=c_sb[:, c * CHUNK : (c + 1) * CHUNK], in_=acc[:])
+            acc = product(banks[c], g_mx, v_mx[0][:], v_mx[1][:])
+            nc.scalar.copy(out=c_sb[:, pieces[c][0] : pieces[c][0] + pieces[c][1]], in_=acc[:])
 
-        neg_xp = sb.tile([P, I], F32, name="neg_xp")
-        neg_xz = sb.tile([P, 1], F32, name="neg_xz")
-        nc.vector.scalar_tensor_tensor(neg_xp[:], sm[:], 1.0, t[:], ALU.subtract, ALU.mult, accum_out=neg_xz[:])
-        neg_p = sb.tile([P, I], F32, name="neg_p")
-        neg_sum = sb.tile([P, 1], F32, name="neg_sum")
-        z = sb.tile([P, 1], F32, name="z")
-        r = sb.tile([P, 1], F32, name="r")
-        neg_xzr = sb.tile([P, 1], F32, name="neg_xzr")
-        gain = sb.tile([P, 1], F32, name="gain")
+        neg_p, neg_sum = slots("neg_p", "v3_bf"), column("neg_sum")
         nc.vector.scalar_tensor_tensor(neg_p[:], neg_a[:], th_sb[:], ln_sm[:], ALU.add, ALU.min, accum_out=neg_sum[:])
+        neg_xp, neg_xz = slots("neg_xp", "v4_bf"), column("neg_xz")
+        nc.vector.scalar_tensor_tensor(neg_xp[:], sm[:], 1.0, t[:], ALU.subtract, ALU.mult, accum_out=neg_xz[:])
+        z, r = column("z"), column("r")
         nc.vector.tensor_scalar(z[:], neg_sum[:], -1.0, res_sb[:], ALU.mult, ALU.add)
-        nc.vector.reciprocal(r[:], z[:])
-        nc.vector.tensor_scalar(neg_xzr[:], neg_xz[:], r[:], None, ALU.mult)
-        nc.vector.tensor_scalar(gain[:], r[:], -1024.0, None, ALU.mult)
-        hx = sb.tile([P, I], F32, name="hx")
-        nc.vector.scalar_tensor_tensor(hx[:], t[:], neg_xzr[:], neg_xp[:], ALU.add, ALU.add)
-        neg_s = sb.tile([P, I], F32, name="neg_s")
-        nc.scalar.activation(out=neg_s[:], in_=sm[:], func=ACT.Copy, bias=-1.0)
-
-        w = sb.tile([P, I], F32, name="w")
+        w = slots("w")
         nc.vector.tensor_copy(w[:], c_sb[:].indirect(offsets[:]))
-        wp = sb.tile([P, I], F32, name="wp")
-        neg_r1 = sb.tile([P, 1], F32, name="neg_r1")
-        nc.vector.scalar_tensor_tensor(wp[:], w[:], r[:], neg_p[:], ALU.mult, ALU.mult, accum_out=neg_r1[:])
-        wx = sb.tile([P, I], F32, name="wx")
-        neg_r2 = sb.tile([P, 1], F32, name="neg_r2")
-        nc.vector.scalar_tensor_tensor(wx[:], w[:], r[:], neg_xp[:], ALU.mult, ALU.mult, accum_out=neg_r2[:])
-        y0 = sb.tile([P, I], F32, name="y0")
-        nc.vector.scalar_tensor_tensor(y0[:], w[:], neg_r1[:], hx[:], ALU.add, ALU.mult)
-        shift = sb.tile([P, 1], F32, name="shift")
-        nc.vector.tensor_scalar(shift[:], neg_r1[:], neg_xzr[:], neg_r2[:], ALU.mult, ALU.add)
-        y = sb.tile([P, I], F32, name="y")
-        nc.vector.tensor_scalar(y[:], y0[:], shift[:], gain[:], ALU.add, ALU.mult)
-        nc.vector.tensor_tensor(placed[:].indirect(offsets[:]), y[:], neg_s[:], ALU.mult)
+        nc.vector.reciprocal(r[:], z[:])
+        neg_xzr, gain, neg_gain = column("neg_xzr"), column("gain"), column("neg_gain")
+        nc.scalar.activation(out=neg_xzr[:], in_=neg_xz[:], func=ACT.Copy, scale=r[:])
+        tx = slots("tx")
+        nc.scalar.activation(out=tx[:], in_=t[:], func=ACT.Identity, bias=neg_xzr[:])
+        nc.scalar.activation(out=gain[:], in_=r[:], func=ACT.Copy, scale=1024.0)
+        nc.scalar.activation(out=neg_gain[:], in_=r[:], func=ACT.Copy, scale=-1024.0)
+        sg = slots("sg")
+        nc.scalar.activation(out=sg[:], in_=sm[:], func=ACT.Identity, scale=neg_gain[:], bias=gain[:])
 
+        wp, neg_r1 = slots("wp"), column("neg_r1")
+        nc.vector.scalar_tensor_tensor(wp[:], w[:], r[:], neg_p[:], ALU.mult, ALU.mult, accum_out=neg_r1[:])
+        neg_vx, neg_d = slots("neg_vx"), column("neg_d")
+        nc.vector.scalar_tensor_tensor(neg_vx[:], w[:], neg_r1[:], neg_xp[:], ALU.add, ALU.mult, accum_out=neg_d[:])
+        vt = slots("vt")
+        nc.vector.scalar_tensor_tensor(vt[:], w[:], neg_r1[:], tx[:], ALU.add, ALU.mult)
+        shift = column("shift")
+        nc.vector.tensor_scalar(shift[:], neg_d[:], r[:], None, ALU.mult)
+        y = slots("y")
+        nc.vector.scalar_tensor_tensor(y[:], vt[:], shift[:], neg_vx[:], ALU.add, ALU.add)
+        nc.vector.tensor_tensor(placed[:].indirect(offsets[:]), y[:], sg[:], ALU.mult)
+
+        edges = (0, 256, 512, 768, T)
         for h in range(4):
-            cols = slice(h * CHUNK, (h + 1) * CHUNK)
-            res = sb.tile([P, CHUNK], F32, name="res%d" % h)
+            cols = slice(edges[h], edges[h + 1])
+            res = sb.tile([P, edges[h + 1] - edges[h]], F32, name="res%d" % h)
             nc.vector.tensor_tensor(res[:], placed[:, cols], base_sb[:, cols], ALU.add)
             (nc.sync if h % 2 == 0 else nc.scalar).dma_start(out=out[:, cols], in_=res[:])

@@ -164,7 +164,9 @@ def tile_attend_hvspotlight_heads_kernel(tc, query, keys_words, keys_scales, gou
         nc.vector.tensor_scalar(shift[:], neg_d[:], r[:], None, ALU.mult)
         y = slots("y")
         nc.vector.scalar_tensor_tensor(y[:], vt[:], shift[:], neg_vx[:], ALU.add, ALU.add)
-        nc.vector.tensor_tensor(placed[:].indirect(offsets[:]), y[:], sg[:], ALU.mult)
+        xe = slots("xe")
+        nc.vector.tensor_tensor(xe[:], y[:], sg[:], ALU.mult)
+        nc.vector.tensor_copy(placed[:].indirect(offsets[:]), xe[:])
 
         edges = (0, 256, 512, 768, T)
         for h in range(4):

@@ -3,7 +3,7 @@ from contextlib import ExitStack
 import concourse.mybir as mybir
 
 D, E, T, Q, I = 512, 512, 1024, 128, 512
-FLOPS = 3 * 2 * D * Q * T
+FLOPS = 2 * Q * T * (2 * D + E)
 
 F32 = mybir.dt.float32
 BF16 = mybir.dt.bfloat16
@@ -17,11 +17,13 @@ ACT = mybir.ActivationFunctionType
 
 P = 128
 PACK = 4
-BANK = 512
-CHUNK = 256
-FLOOR = 2.0 ** -50
-RUN = 2
-SHARE = 96
+HALF = T // 2
+CHUNK = T // 4
+PAIR = 2
+SCALAR_SHARE = 96
+FLOOR_AT = -35.0
+GAIN = 1024.0
+ALIGN = 64
 
 
 def tile_attend_hvspotlight_heads_kernel(tc, query, keys_words, keys_scales, gout, vals, th, reserve, dquery, base, offs, out):
@@ -33,65 +35,66 @@ def tile_attend_hvspotlight_heads_kernel(tc, query, keys_words, keys_scales, gou
         def column(name):
             return sb.tile([P, 1], F32, name=name)
 
-        def slots(name, tag=""):
-            return sb.tile([P, I], F32, name=name, tag=tag or name, align_bytes=64)
+        def slots(name, buffer=""):
+            return sb.tile([P, I], F32, name=name, tag=buffer or name, align_bytes=ALIGN)
 
         def load_rows(name, rows):
-            raw = sb.tile([P, PACK, rows.shape[1]], F32, name=name + "_raw", tag=name + "_raw", align_bytes=64)
+            raw = sb.tile([P, PACK, rows.shape[1]], F32, name=name + "_raw", tag=name + "_raw", align_bytes=ALIGN)
             nc.sync.dma_start(out=raw[:], in_=rows.rearrange("(p j) w -> p j w", j=PACK))
             return raw
 
         def grouped_tile(name, width):
-            return sb.tile([P, width, PACK], BF16, name=name + "_bf", tag=name + "_bf", align_bytes=64)
+            return sb.tile([P, width, PACK], BF16, name=name + "_bf", tag=name + "_bf", align_bytes=ALIGN)
 
         def interleave(grouped, raw, on_vector):
-            dst = grouped.rearrange("p (c i) j -> p c j i", i=RUN)
-            src = raw.rearrange("p j (c i) -> p c j i", i=RUN)
+            dst = grouped.rearrange("p (c i) j -> p c j i", i=PAIR)
+            src = raw.rearrange("p j (c i) -> p c j i", i=PAIR)
             if on_vector:
                 nc.vector.tensor_copy(out=dst, in_=src)
             else:
                 nc.scalar.copy(out=dst, in_=src)
 
-        def vector_operand(name, raw):
-            grouped = grouped_tile(name, raw.shape[2])
-            interleave(grouped[:], raw, True)
-            return quantize(name, grouped)
-
         def quantize(name, grouped):
             width = grouped.shape[1]
-            codes = sb.tile([P, width], U32, name=name + "_codes", align_bytes=64)
-            scales = sb.tile([P, width], U8, name=name + "_scales", align_bytes=64)
+            codes = sb.tile([P, width], U32, name=name + "_codes", align_bytes=ALIGN)
+            scales = sb.tile([P, width], U8, name=name + "_scales", align_bytes=ALIGN)
             nc.vector.quantize_mx(out=codes[:].bitcast(FP8X4), scales=scales[:], in_=grouped[:].rearrange("p w j -> p (w j)"))
             return codes, scales
 
-        def product(bank, lhs, rhs_codes, rhs_scales):
-            acc = ps.tile([P, rhs_codes.shape[1]], F32, name=bank)
-            nc.tensor.matmul_mx(out=acc[:], lhsT=lhs[0][:].bitcast(FP8X4), lhsT_scale=lhs[1][:],
-                                rhs=rhs_codes.bitcast(FP8X4), rhs_scale=rhs_scales, start=True, stop=True)
-            return acc
+        def stationary_operand(name, raw):
+            grouped = grouped_tile(name, Q)
+            interleave(grouped[:], raw[:], True)
+            return quantize(name, grouped)
 
-        k_scales = sb.tile([P, T], U8, name="k_scales", align_bytes=64)
+        def product_to(window, bank, stationary, codes, scales):
+            acc = ps.tile([P, codes.shape[1]], F32, name=bank)
+            nc.tensor.matmul_mx(out=acc[:], lhsT=stationary[0][:].bitcast(FP8X4), lhsT_scale=stationary[1][:],
+                                rhs=codes.bitcast(FP8X4), rhs_scale=scales, start=True, stop=True)
+            nc.scalar.copy(out=window, in_=acc[:])
+
+        k_scales = sb.tile([P, T], U8, name="k_scales", align_bytes=ALIGN)
         nc.vector.memset(k_scales[:].bitcast(I32), 0)
-        warm = sb.tile([P, 2], F32, name="warm")
-        nc.vector.memset(warm[:, 0:1], 0.0)
+        floor = sb.tile([P, 2], F32, name="floor")
+        nc.vector.memset(floor[:, 0:1], FLOOR_AT)
         placed = sb.tile([P, T], F32, name="placed")
         nc.vector.memset(placed[:], 0.0)
 
         for g in range(4):
-            (nc.scalar if g < 2 else nc.sync).dma_start(out=k_scales[32 * g : 32 * g + 4, :].bitcast(I32), in_=keys_scales[0, 4 * g : 4 * g + 4, :].bitcast(I32))
+            queue = nc.scalar if g < 2 else nc.sync
+            queue.dma_start(out=k_scales[32 * g : 32 * g + 4, :].bitcast(I32), in_=keys_scales[0, 4 * g : 4 * g + 4, :].bitcast(I32))
         q_raw = load_rows("q", query)
-        k_words = keys_words[0].rearrange("p n t -> p (n t)").bitcast(I32)
+        k_words = keys_words[0].rearrange("p n j -> p (n j)").bitcast(I32)
         k_codes = []
         for h in range(2):
-            half = sb.tile([P, BANK], U32, name="k_codes%d" % h, align_bytes=64)
-            nc.sync.dma_start(out=half[:].bitcast(I32), in_=k_words[:, h * BANK : (h + 1) * BANK])
-            k_codes.append(half)
+            k_half = sb.tile([P, HALF], U32, name="k_codes%d" % h, align_bytes=ALIGN)
+            nc.sync.dma_start(out=k_half[:].bitcast(I32), in_=k_words[:, h * HALF : (h + 1) * HALF])
+            k_codes.append(k_half)
         dq_raw = load_rows("dq", dquery)
-        nc.scalar.activation(out=warm[:, 1:2], in_=warm[:, 0:1], func=ACT.Sigmoid)
+        nc.scalar.activation(out=floor[:, 1:2], in_=floor[:, 0:1], func=ACT.Sigmoid)
         th_sb = column("th_sb")
         nc.gpsimd.dma_start(out=th_sb[:], in_=th)
-        res_sb = column("res_sb")
-        nc.gpsimd.dma_start(out=res_sb[:], in_=reserve)
+        reserve_sb = column("reserve_sb")
+        nc.gpsimd.dma_start(out=reserve_sb[:], in_=reserve)
         g_raw = load_rows("g", gout)
         offsets = sb.tile([P, I // 16], U16, name="offsets")
         nc.sync.dma_start(offsets[:], offs)
@@ -99,78 +102,76 @@ def tile_attend_hvspotlight_heads_kernel(tc, query, keys_words, keys_scales, gou
         base_sb = sb.tile([P, T], F32, name="base_sb")
         nc.sync.dma_start(out=base_sb[:], in_=base)
 
-        q_mx = vector_operand("q", q_raw[:])
+        q_mx = stationary_operand("q", q_raw)
         a_sb = sb.tile([P, T], F32, name="a_sb")
         for c in range(T // CHUNK):
             cols = slice(c * CHUNK, (c + 1) * CHUNK)
-            acc = product("quarter%d" % c, q_mx, k_codes[c // 2][:, (c % 2) * CHUNK : (c % 2 + 1) * CHUNK], k_scales[:, cols])
-            nc.scalar.copy(out=a_sb[:, cols], in_=acc[:])
-        dq_mx = vector_operand("dq", dq_raw[:])
+            product_to(a_sb[:, cols], "quarter%d" % c, q_mx, k_codes[c // 2][:, (c % 2) * CHUNK : (c % 2 + 1) * CHUNK], k_scales[:, cols])
+        dq_mx = stationary_operand("dq", dq_raw)
         ta_sb = sb.tile([P, T], F32, name="ta_sb")
         for h in range(2):
-            acc = product("half%d" % h, dq_mx, k_codes[h][:], k_scales[:, h * BANK : (h + 1) * BANK])
-            nc.scalar.copy(out=ta_sb[:, h * BANK : (h + 1) * BANK], in_=acc[:])
+            cols = slice(h * HALF, (h + 1) * HALF)
+            product_to(ta_sb[:, cols], "half%d" % h, dq_mx, k_codes[h][:], k_scales[:, cols])
 
         neg_a = slots("neg_a")
         nc.vector.tensor_scalar(neg_a[:], a_sb[:].indirect(offsets[:]), -1.0, 0.0, ALU.mult, ALU.add)
-        pieces = [(0, CHUNK), (CHUNK, CHUNK), (2 * CHUNK, CHUNK), (3 * CHUNK, P), (3 * CHUNK + P, P)]
-        v_bf = [grouped_tile("v%d" % c, pieces[c][1]) for c in range(5)]
+
+        pieces = [(0, CHUNK), (CHUNK, CHUNK), (2 * CHUNK, CHUNK), (3 * CHUNK, CHUNK // 2), (3 * CHUNK + CHUNK // 2, CHUNK // 2)]
+        v_bf = [grouped_tile("v%d" % n, width) for n, (first, width) in enumerate(pieces)]
         interleave(v_bf[0][:], v_raw[0][:], False)
         sm = slots("sm")
         nc.scalar.activation(out=sm[:], in_=neg_a[:], func=ACT.Sigmoid, bias=th_sb[:])
-        interleave(v_bf[1][:, 0:SHARE, :], v_raw[1][:, :, 0:SHARE], False)
+        interleave(v_bf[1][:, 0:SCALAR_SHARE, :], v_raw[1][:, :, 0:SCALAR_SHARE], False)
 
         t = slots("t")
         nc.vector.tensor_copy(t[:], ta_sb[:].indirect(offsets[:]))
-        g_mx = vector_operand("g", g_raw[:])
-        interleave(v_bf[1][:, SHARE:CHUNK, :], v_raw[1][:, :, SHARE:CHUNK], True)
+        g_mx = stationary_operand("g", g_raw)
+        interleave(v_bf[1][:, SCALAR_SHARE:CHUNK, :], v_raw[1][:, :, SCALAR_SHARE:CHUNK], True)
         ln_sm = slots("ln_sm", "v1_raw")
-        nc.scalar.activation(out=ln_sm[:], in_=sm[:], func=ACT.Ln, bias=FLOOR)
+        nc.scalar.activation(out=ln_sm[:], in_=sm[:], func=ACT.Ln, bias=floor[:, 1:2])
         interleave(v_bf[2][:], v_raw[2][:], True)
-        interleave(v_bf[3][:], v_raw[3][:, :, 0:P], True)
-        interleave(v_bf[4][:], v_raw[3][:, :, P:CHUNK], True)
+        interleave(v_bf[3][:], v_raw[3][:, :, 0 : CHUNK // 2], True)
+        interleave(v_bf[4][:], v_raw[3][:, :, CHUNK // 2 : CHUNK], True)
         c_sb = sb.tile([P, T], F32, name="c_sb")
         banks = ["quarter0", "quarter1", "quarter2", "quarter3", "half0"]
-        for c in range(5):
-            v_mx = quantize("v%d" % c, v_bf[c])
-            acc = product(banks[c], g_mx, v_mx[0][:], v_mx[1][:])
-            nc.scalar.copy(out=c_sb[:, pieces[c][0] : pieces[c][0] + pieces[c][1]], in_=acc[:])
+        for n, (first, width) in enumerate(pieces):
+            v_codes, v_scales = quantize("v%d" % n, v_bf[n])
+            product_to(c_sb[:, first : first + width], banks[n], g_mx, v_codes[:], v_scales[:])
 
-        neg_p, neg_sum = slots("neg_p", "v3_bf"), column("neg_sum")
-        nc.vector.scalar_tensor_tensor(neg_p[:], neg_a[:], th_sb[:], ln_sm[:], ALU.add, ALU.min, accum_out=neg_sum[:])
+        neg_p, neg_p_sum = slots("neg_p", "v3_bf"), column("neg_p_sum")
+        nc.vector.scalar_tensor_tensor(neg_p[:], neg_a[:], th_sb[:], ln_sm[:], ALU.add, ALU.min, accum_out=neg_p_sum[:])
         neg_xp, neg_xz = slots("neg_xp", "v4_bf"), column("neg_xz")
         nc.vector.scalar_tensor_tensor(neg_xp[:], sm[:], 1.0, t[:], ALU.subtract, ALU.mult, accum_out=neg_xz[:])
         z, r = column("z"), column("r")
-        nc.vector.tensor_scalar(z[:], neg_sum[:], -1.0, res_sb[:], ALU.mult, ALU.add)
+        nc.vector.tensor_scalar(z[:], neg_p_sum[:], -1.0, reserve_sb[:], ALU.mult, ALU.add)
         w = slots("w")
         nc.vector.tensor_copy(w[:], c_sb[:].indirect(offsets[:]))
         nc.vector.reciprocal(r[:], z[:])
-        neg_xzr, gain, neg_gain = column("neg_xzr"), column("gain"), column("neg_gain")
-        nc.scalar.activation(out=neg_xzr[:], in_=neg_xz[:], func=ACT.Copy, scale=r[:])
-        tx = slots("tx")
-        nc.scalar.activation(out=tx[:], in_=t[:], func=ACT.Identity, bias=neg_xzr[:])
-        nc.scalar.activation(out=gain[:], in_=r[:], func=ACT.Copy, scale=1024.0)
-        nc.scalar.activation(out=neg_gain[:], in_=r[:], func=ACT.Copy, scale=-1024.0)
-        sg = slots("sg")
-        nc.scalar.activation(out=sg[:], in_=sm[:], func=ACT.Identity, scale=neg_gain[:], bias=gain[:])
 
-        wp, neg_r1 = slots("wp"), column("neg_r1")
-        nc.vector.scalar_tensor_tensor(wp[:], w[:], r[:], neg_p[:], ALU.mult, ALU.mult, accum_out=neg_r1[:])
-        neg_vx, neg_d = slots("neg_vx"), column("neg_d")
-        nc.vector.scalar_tensor_tensor(neg_vx[:], w[:], neg_r1[:], neg_xp[:], ALU.add, ALU.mult, accum_out=neg_d[:])
-        vt = slots("vt")
-        nc.vector.scalar_tensor_tensor(vt[:], w[:], neg_r1[:], tx[:], ALU.add, ALU.mult)
+        neg_r_xz, gain_r, neg_gain_r = column("neg_r_xz"), column("gain_r"), column("neg_gain_r")
+        nc.scalar.activation(out=neg_r_xz[:], in_=neg_xz[:], func=ACT.Copy, scale=r[:])
+        nc.scalar.activation(out=gain_r[:], in_=r[:], func=ACT.Copy, scale=GAIN)
+        nc.scalar.activation(out=neg_gain_r[:], in_=r[:], func=ACT.Copy, scale=-GAIN)
+        gain_r_s = slots("gain_r_s")
+        nc.scalar.activation(out=gain_r_s[:], in_=sm[:], func=ACT.Identity, scale=neg_gain_r[:], bias=gain_r[:])
+
+        wp_terms, neg_mean = slots("wp_terms"), column("neg_mean")
+        nc.vector.scalar_tensor_tensor(wp_terms[:], w[:], r[:], neg_p[:], ALU.mult, ALU.mult, accum_out=neg_mean[:])
+        centred = slots("centred")
+        nc.vector.scalar_tensor_tensor(centred[:], t[:], neg_r_xz[:], neg_xp[:], ALU.add, ALU.add)
+        vxp_terms, neg_vxp = slots("vxp_terms"), column("neg_vxp")
+        nc.vector.scalar_tensor_tensor(vxp_terms[:], w[:], neg_mean[:], neg_xp[:], ALU.add, ALU.mult, accum_out=neg_vxp[:])
+        v_centred = slots("v_centred")
+        nc.vector.scalar_tensor_tensor(v_centred[:], w[:], neg_mean[:], centred[:], ALU.add, ALU.mult)
         shift = column("shift")
-        nc.vector.tensor_scalar(shift[:], neg_d[:], r[:], None, ALU.mult)
-        y = slots("y")
-        nc.vector.scalar_tensor_tensor(y[:], vt[:], shift[:], neg_vx[:], ALU.add, ALU.add)
+        nc.scalar.activation(out=shift[:], in_=neg_vxp[:], func=ACT.Copy, scale=r[:])
         xe = slots("xe")
-        nc.vector.tensor_tensor(xe[:], y[:], sg[:], ALU.mult)
+        nc.vector.scalar_tensor_tensor(xe[:], v_centred[:], shift[:], gain_r_s[:], ALU.add, ALU.mult)
         nc.vector.tensor_copy(placed[:].indirect(offsets[:]), xe[:])
 
-        edges = (0, 256, 512, 768, T)
-        for h in range(4):
-            cols = slice(edges[h], edges[h + 1])
-            res = sb.tile([P, edges[h + 1] - edges[h]], F32, name="res%d" % h)
-            nc.vector.tensor_tensor(res[:], placed[:, cols], base_sb[:, cols], ALU.add)
-            (nc.sync if h % 2 == 0 else nc.scalar).dma_start(out=out[:, cols], in_=res[:])
+        for c in range(T // CHUNK):
+            cols = slice(c * CHUNK, (c + 1) * CHUNK)
+            result = sb.tile([P, CHUNK], F32, name="result%d" % c)
+            nc.vector.tensor_tensor(result[:], placed[:, cols], base_sb[:, cols], ALU.add)
+            queue = nc.sync if c % 2 == 0 else nc.scalar
+            queue.dma_start(out=out[:, cols], in_=result[:])

from contextlib import ExitStack

import concourse.mybir as mybir

D, E, T, Q, I = 512, 512, 1024, 128, 512
FLOPS = 2 * Q * T * (2 * D + E)

F32 = mybir.dt.float32
BF16 = mybir.dt.bfloat16
I32 = mybir.dt.int32
U32 = mybir.dt.uint32
U16 = mybir.dt.uint16
U8 = mybir.dt.uint8
FP8X4 = mybir.dt.float8_e4m3fn_x4
ALU = mybir.AluOpType
ACT = mybir.ActivationFunctionType

P = 128
PACK = 4
HALF = T // 2
CHUNK = T // 4
PAIR = 2
SCALAR_SHARE = 96
FLOOR_AT = -35.0
GAIN = 1024.0
ALIGN = 64


def tile_attend_hvspotlight_heads_kernel(tc, query, keys_words, keys_scales, gout, vals, th, reserve, dquery, base, offs, out):
    nc = tc.nc
    with ExitStack() as ctx:
        sb = ctx.enter_context(tc.tile_pool(name="sb", bufs=1))
        ps = ctx.enter_context(tc.psum_pool(name="ps", bufs=1))

        def column(name):
            return sb.tile([P, 1], F32, name=name)

        def slots(name, buffer=""):
            return sb.tile([P, I], F32, name=name, tag=buffer or name, align_bytes=ALIGN)

        def load_rows(name, rows):
            raw = sb.tile([P, PACK, rows.shape[1]], F32, name=name + "_raw", tag=name + "_raw", align_bytes=ALIGN)
            nc.sync.dma_start(out=raw[:], in_=rows.rearrange("(p j) w -> p j w", j=PACK))
            return raw

        def grouped_tile(name, width):
            return sb.tile([P, width, PACK], BF16, name=name + "_bf", tag=name + "_bf", align_bytes=ALIGN)

        def interleave(grouped, raw, on_vector):
            dst = grouped.rearrange("p (c i) j -> p c j i", i=PAIR)
            src = raw.rearrange("p j (c i) -> p c j i", i=PAIR)
            if on_vector:
                nc.vector.tensor_copy(out=dst, in_=src)
            else:
                nc.scalar.copy(out=dst, in_=src)

        def quantize(name, grouped):
            width = grouped.shape[1]
            codes = sb.tile([P, width], U32, name=name + "_codes", align_bytes=ALIGN)
            scales = sb.tile([P, width], U8, name=name + "_scales", align_bytes=ALIGN)
            nc.vector.quantize_mx(out=codes[:].bitcast(FP8X4), scales=scales[:], in_=grouped[:].rearrange("p w j -> p (w j)"))
            return codes, scales

        def stationary_operand(name, raw):
            grouped = grouped_tile(name, Q)
            interleave(grouped[:], raw[:], True)
            return quantize(name, grouped)

        def product_to(window, bank, stationary, codes, scales):
            acc = ps.tile([P, codes.shape[1]], F32, name=bank)
            nc.tensor.matmul_mx(out=acc[:], lhsT=stationary[0][:].bitcast(FP8X4), lhsT_scale=stationary[1][:],
                                rhs=codes.bitcast(FP8X4), rhs_scale=scales, start=True, stop=True)
            nc.scalar.copy(out=window, in_=acc[:])

        k_scales = sb.tile([P, T], U8, name="k_scales", align_bytes=ALIGN)
        nc.vector.memset(k_scales[:].bitcast(I32), 0)
        floor = sb.tile([P, 2], F32, name="floor")
        nc.vector.memset(floor[:, 0:1], FLOOR_AT)
        placed = sb.tile([P, T], F32, name="placed")
        nc.vector.memset(placed[:], 0.0)

        for g in range(4):
            queue = nc.scalar if g < 2 else nc.sync
            queue.dma_start(out=k_scales[32 * g : 32 * g + 4, :].bitcast(I32), in_=keys_scales[0, 4 * g : 4 * g + 4, :].bitcast(I32))
        q_raw = load_rows("q", query)
        k_words = keys_words[0].rearrange("p n j -> p (n j)").bitcast(I32)
        k_codes = []
        for h in range(2):
            k_half = sb.tile([P, HALF], U32, name="k_codes%d" % h, align_bytes=ALIGN)
            nc.sync.dma_start(out=k_half[:].bitcast(I32), in_=k_words[:, h * HALF : (h + 1) * HALF])
            k_codes.append(k_half)
        dq_raw = load_rows("dq", dquery)
        nc.scalar.activation(out=floor[:, 1:2], in_=floor[:, 0:1], func=ACT.Sigmoid)
        th_sb = column("th_sb")
        nc.gpsimd.dma_start(out=th_sb[:], in_=th)
        reserve_sb = column("reserve_sb")
        nc.gpsimd.dma_start(out=reserve_sb[:], in_=reserve)
        g_raw = load_rows("g", gout)
        offsets = sb.tile([P, I // 16], U16, name="offsets")
        nc.sync.dma_start(offsets[:], offs)
        v_raw = [load_rows("v%d" % c, vals[:, c * CHUNK : (c + 1) * CHUNK]) for c in range(T // CHUNK)]
        base_sb = sb.tile([P, T], F32, name="base_sb")
        nc.sync.dma_start(out=base_sb[:], in_=base)

        q_mx = stationary_operand("q", q_raw)
        a_sb = sb.tile([P, T], F32, name="a_sb")
        for c in range(T // CHUNK):
            cols = slice(c * CHUNK, (c + 1) * CHUNK)
            product_to(a_sb[:, cols], "quarter%d" % c, q_mx, k_codes[c // 2][:, (c % 2) * CHUNK : (c % 2 + 1) * CHUNK], k_scales[:, cols])
        dq_mx = stationary_operand("dq", dq_raw)
        ta_sb = sb.tile([P, T], F32, name="ta_sb")
        for h in range(2):
            cols = slice(h * HALF, (h + 1) * HALF)
            product_to(ta_sb[:, cols], "half%d" % h, dq_mx, k_codes[h][:], k_scales[:, cols])

        neg_a = slots("neg_a")
        nc.vector.tensor_scalar(neg_a[:], a_sb[:].indirect(offsets[:]), -1.0, 0.0, ALU.mult, ALU.add)

        pieces = [(0, CHUNK), (CHUNK, CHUNK), (2 * CHUNK, CHUNK), (3 * CHUNK, CHUNK // 2), (3 * CHUNK + CHUNK // 2, CHUNK // 2)]
        v_bf = [grouped_tile("v%d" % n, width) for n, (first, width) in enumerate(pieces)]
        interleave(v_bf[0][:], v_raw[0][:], False)
        sm = slots("sm")
        nc.scalar.activation(out=sm[:], in_=neg_a[:], func=ACT.Sigmoid, bias=th_sb[:])
        interleave(v_bf[1][:, 0:SCALAR_SHARE, :], v_raw[1][:, :, 0:SCALAR_SHARE], False)

        t = slots("t")
        nc.vector.tensor_copy(t[:], ta_sb[:].indirect(offsets[:]))
        g_mx = stationary_operand("g", g_raw)
        interleave(v_bf[1][:, SCALAR_SHARE:CHUNK, :], v_raw[1][:, :, SCALAR_SHARE:CHUNK], True)
        ln_sm = slots("ln_sm", "v1_raw")
        nc.scalar.activation(out=ln_sm[:], in_=sm[:], func=ACT.Ln, bias=floor[:, 1:2])
        interleave(v_bf[2][:], v_raw[2][:], True)
        interleave(v_bf[3][:], v_raw[3][:, :, 0 : CHUNK // 2], True)
        interleave(v_bf[4][:], v_raw[3][:, :, CHUNK // 2 : CHUNK], True)
        c_sb = sb.tile([P, T], F32, name="c_sb")
        banks = ["quarter0", "quarter1", "quarter2", "quarter3", "half0"]
        for n, (first, width) in enumerate(pieces):
            v_codes, v_scales = quantize("v%d" % n, v_bf[n])
            product_to(c_sb[:, first : first + width], banks[n], g_mx, v_codes[:], v_scales[:])

        neg_p, neg_p_sum = slots("neg_p", "v3_bf"), column("neg_p_sum")
        nc.vector.scalar_tensor_tensor(neg_p[:], neg_a[:], th_sb[:], ln_sm[:], ALU.add, ALU.min, accum_out=neg_p_sum[:])
        neg_xp, neg_xz = slots("neg_xp", "v4_bf"), column("neg_xz")
        nc.vector.scalar_tensor_tensor(neg_xp[:], sm[:], 1.0, t[:], ALU.subtract, ALU.mult, accum_out=neg_xz[:])
        z, r = column("z"), column("r")
        nc.vector.tensor_scalar(z[:], neg_p_sum[:], -1.0, reserve_sb[:], ALU.mult, ALU.add)
        w = slots("w")
        nc.vector.tensor_copy(w[:], c_sb[:].indirect(offsets[:]))
        nc.vector.reciprocal(r[:], z[:])

        neg_r_xz, gain_r, neg_gain_r = column("neg_r_xz"), column("gain_r"), column("neg_gain_r")
        nc.scalar.activation(out=neg_r_xz[:], in_=neg_xz[:], func=ACT.Copy, scale=r[:])
        nc.scalar.activation(out=gain_r[:], in_=r[:], func=ACT.Copy, scale=GAIN)
        nc.scalar.activation(out=neg_gain_r[:], in_=r[:], func=ACT.Copy, scale=-GAIN)
        gain_r_s = slots("gain_r_s")
        nc.scalar.activation(out=gain_r_s[:], in_=sm[:], func=ACT.Identity, scale=neg_gain_r[:], bias=gain_r[:])

        wp_terms, neg_mean = slots("wp_terms"), column("neg_mean")
        nc.vector.scalar_tensor_tensor(wp_terms[:], w[:], r[:], neg_p[:], ALU.mult, ALU.mult, accum_out=neg_mean[:])
        centred = slots("centred")
        nc.vector.scalar_tensor_tensor(centred[:], t[:], neg_r_xz[:], neg_xp[:], ALU.add, ALU.add)
        vxp_terms, neg_vxp = slots("vxp_terms"), column("neg_vxp")
        nc.vector.scalar_tensor_tensor(vxp_terms[:], w[:], neg_mean[:], neg_xp[:], ALU.add, ALU.mult, accum_out=neg_vxp[:])
        v_centred = slots("v_centred")
        nc.vector.scalar_tensor_tensor(v_centred[:], w[:], neg_mean[:], centred[:], ALU.add, ALU.mult)
        shift = column("shift")
        nc.scalar.activation(out=shift[:], in_=neg_vxp[:], func=ACT.Copy, scale=r[:])
        xe = slots("xe")
        nc.vector.scalar_tensor_tensor(xe[:], v_centred[:], shift[:], gain_r_s[:], ALU.add, ALU.mult)
        nc.vector.tensor_copy(placed[:].indirect(offsets[:]), xe[:])

        for c in range(T // CHUNK):
            cols = slice(c * CHUNK, (c + 1) * CHUNK)
            result = sb.tile([P, CHUNK], F32, name="result%d" % c)
            nc.vector.tensor_tensor(result[:], placed[:, cols], base_sb[:, cols], ALU.add)
            queue = nc.sync if c % 2 == 0 else nc.scalar
            queue.dma_start(out=out[:, cols], in_=result[:])
